import numpy as np, ml_dtypes
CORES = [23,119,17,113]
N = 4
import mx_ref
BF = ml_dtypes.bfloat16
def rowtile(v, k):
    z = np.concatenate([v, np.zeros((1, v.shape[1]), BF)])
    return np.concatenate([np.ascontiguousarray(z[k[:, 4 * m:4 * m + 4]].transpose(0, 2, 1)).reshape(128, -1) for m in range(k.shape[1] // 4)], axis=1)
def cut(t, i, w=512):
    return t[:, w * i:w * i + w]
def f(rng, *shape):
    return mx_ref.flush((rng.standard_normal(shape, dtype=np.float32) * np.exp2(rng.integers(-2, 3, shape[:-1] + (1,)))).astype(BF))
def wide(rng, *shape, cols=0):
    v = rng.standard_normal(shape, dtype=np.float32) * np.exp2(rng.integers(-12, 13, shape)).astype(np.float32)
    if cols: v *= np.repeat(np.exp2(rng.integers(-cols, cols + 1, shape[:-2] + (1, shape[-1] // 4))) * (rng.random(shape[:-2] + (1, shape[-1] // 4)) > 0.0625), 4, axis=-1).astype(np.float32)
    return mx_ref.flush(v.astype(BF))
T, GW, CAPP = 1024, 1024, 256
def counts(rng):
    n = rng.integers(0, CAPP + 1, (N, N))
    for e in range(N):
        if n[:, e].sum() < CAPP: n[rng.integers(0, N), e] = CAPP
    return n
def lists(rng, n):
    l = np.full((N, N, 512), -1)
    for s in range(N):
        for e in range(N): l[s, e, :n[s, e]] = rng.integers(0, T, n[s, e])
    return l
def store(l):
    return np.ascontiguousarray(l.reshape(N, N, 128, 4).transpose(0, 2, 1, 3)).reshape(N, 128, 4 * N).astype(np.int32)
def setup_inputs(rng):
    return {"x": f(rng, N, T, 128), "dy": f(rng, N, T, GW), "pick": store(lists(rng, counts(rng)))}
def setup_inputs_alike(rng):
    d = setup_inputs(rng); l = np.full((N, N, 512), -1); n = rng.integers(CAPP // 2, CAPP + 1)
    l[:, :, :n] = rng.integers(0, T, n)
    d["pick"] = store(l); return d
def setup_inputs_counts(rng):
    d = setup_inputs(rng)
    n = np.array([0, 1, 33, CAPP])[(np.arange(N)[:, None] + np.arange(N) + rng.integers(0, 4)) % 4][rng.permutation(N)]
    d["pick"] = store(lists(rng, n)); return d
def setup_inputs_giant(rng):
    d = setup_inputs(rng); l = lists(rng, rng.integers(64, CAPP + 1, (N, N)))
    for s in range(N):
        k = rng.permutation(T); kx, kg = k[:T // 32], k[T // 32:T // 16]
        d["x"][s, kx] = (d["x"][s, kx].astype(np.float32) * np.float32(4096)).astype(BF)
        d["dy"][s, kg] = (d["dy"][s, kg].astype(np.float32) * np.float32(4096)).astype(BF)
        for e in range(N):
            i = rng.permutation(32)
            l[s, e, i[0]], l[s, e, i[1]] = rng.choice(kx), rng.choice(kg)
    d["pick"] = store(l); return d
def setup_inputs_reversed(rng):
    d = setup_inputs(rng); n = counts(rng); l = lists(rng, n)
    for s in range(N):
        for e in range(N): l[s, e, :n[s, e]] = np.sort(l[s, e, :n[s, e]])[::-1]
    d["pick"] = store(l); return d
def setup_inputs_spread(rng):
    d = setup_inputs(rng); d["x"] = wide(rng, N, T, 128); d["dy"] = wide(rng, N, T, GW)
    d["pick"] = store(lists(rng, rng.integers(CAPP // 2, CAPP + 1, (N, N)))); return d
def check_inputs(d):
    b = []
    for q in ("x", "dy"):
        v = np.abs(np.asarray(d[q]).astype(np.float32))
        if not np.isfinite(v).all() or ((v != 0) & ((v < 2.0 ** -30) | (v > 2.0 ** 30))).any(): b.append(q)
    for s in range(N):
        for e in range(N):
            k = np.asarray(d["pick"][s])[:, 4 * e:4 * e + 4].reshape(-1); n = int((k >= 0).sum())
            if n > CAPP or k.max() >= T or (k[:n] < 0).any() or (k[n:] != -1).any(): b.append("pick")
    return b
def reference(x, dy, pick):
    y = np.zeros((N, 128, GW), np.float32)
    for e in range(N):
        for s in range(N):
            k = pick[s][:, 4 * e:4 * e + 4]
            X, G = mx_ref.quantize(rowtile(x[s], k)), rowtile(dy[s], k)
            for i in range(GW // 512): y[e][:, 512 * i:512 * i + 512] += mx_ref.matmul(X, mx_ref.quantize(cut(G, i, 2048)))
    return {"y": y}

@@ -1,0 +1,250 @@
+from concourse.bass import DstId, RemoteDMATransfer, IndirectOffsetOnAxis
+from concourse.mybir import dt, ActivationFunctionType
+
+TOK, XW, GW = 1024, 128, 1024
+JW = XW + GW
+HALF = GW // 2
+QUADS = 64
+COLS = HALF + 2 * XW
+MID = COLS // 2
+
+SCRATCH = {
+    "tab": ("dram", [TOK, JW], "bfloat16"),
+    "idx": ("sbuf", [128, 16], "int32"),
+    "rx0": ("sbuf", [128, 2 * XW], "bfloat16"),
+    "rd0": ("sbuf", [128, 2 * GW], "bfloat16"),
+    "ys": ("sbuf", [128, GW], "float32"),
+    "acc": ("psum", [128, GW], "float32"),
+}
+for _s in range(4):
+    if _s:
+        SCRATCH["rj%d" % _s] = ("sbuf", [128, 2 * JW], "bfloat16")
+    SCRATCH["gt%d" % _s] = ("sbuf", [128, 4 * HALF], "bfloat16")
+    SCRATCH["xt%d" % _s] = ("sbuf", [128, 8 * XW], "bfloat16")
+    SCRATCH["oc%d" % _s] = ("sbuf", [128, COLS], "float8_e4m3fn_x4")
+    SCRATCH["op%d" % _s] = ("sbuf", [128, COLS], "uint8")
+    SCRATCH["ic%d" % _s] = ("sbuf", [128, COLS], "float8_e4m3fn_x4")
+    SCRATCH["ip%d" % _s] = ("sbuf", [128, COLS], "uint8")
+
+SEMAPHORES = ["idx", "ta", "tb", "tc", "td", "tx", "ma", "mb", "mx", "m1", "m2", "m3", "sent",
+              "mm0", "mm1", "ev0", "ev1", "st0", "st1", "x0_0", "x0_1"]
+for _s in range(4):
+    SEMAPHORES += ["g%d_0" % _s, "g%d_1" % _s, "zx%d" % _s]
+    SEMAPHORES += ["sg%d" % _s, "sx%d" % _s, "vg%d" % _s, "vx%d" % _s]
+    SEMAPHORES += ["qg%d" % _s, "qx%d" % _s, "arr%d" % _s]
+
+
+def bits(engines):
+    return sum(1 << e for e in engines)
+
+
+def rank_program(g, core, T, topo):
+    r = T.rank_of(core)
+    if r is None:
+        return
+    cores = T.cores
+    n = len(cores)
+    sem = T.sem
+
+    def here(s):
+        return [e for e in range(n) if topo.chip(cores[e]) == topo.chip(cores[s])]
+
+    def far_order(s):
+        off = [e for e in range(n) if e not in here(s)]
+        return off if here(s)[0] == s else off[::-1]
+
+    far = far_order(r)
+    near = [e for e in here(r) if e != r][0]
+    slot = far + [near, r]
+    early = [s for s in far if far_order(s)[0] == r][0]
+    late = [s for s in far if s != early][0]
+
+    far_eng = topo.engines(core, cores[far[0]])
+    near_eng = [e for e in topo.engines(core, cores[near]) if e not in far_eng]
+
+    g.sync.dma_start(T.idx[0:QUADS, 0:15], T.pick[0:QUADS, 0:15]).then_inc(sem.idx, 16)
+    g.scalar.dma_start(T.idx[QUADS:128, 0:15], T.pick[0:QUADS, 1:16]).then_inc(sem.idx, 16)
+
+    def tab_dy(j, name):
+        g.sync.dma_start(T.tab[128 * j:128 * j + 128, XW:JW], T.dy[128 * j:128 * j + 128, :]).then_inc(sem[name], 16)
+
+    g.dma_start(T.tab[:, 0:XW], T.x[:, :]).then_inc(sem.tx, 16)
+    for j in (0, 1, 2):
+        tab_dy(j, "ta")
+    tab_dy(3, "tb")
+    g.sync.wait_ge(sem.ta, 48)
+    tab_dy(4, "tc")
+    tab_dy(5, "tc")
+    g.sync.wait_ge(sem.tb, 16)
+    tab_dy(6, "td")
+    tab_dy(7, "td")
+
+    def gather(kind, s, u):
+        c = 4 * slot[s] + 2 * u
+        if kind == "x":
+            land, table = T.rx0[:, u * XW:(u + 1) * XW], T.x[:]
+        elif s == 0:
+            land, table = T.rd0[:, u * GW:(u + 1) * GW], T.dy[:]
+        else:
+            land, table = T["rj%d" % s][:, u * JW:(u + 1) * JW], T.tab[:]
+        g.indirect_dma_start(land, None, table, IndirectOffsetOnAxis(ap=T.idx[:, c:c + 1], axis=0),
+                             bounds_check=TOK - 1, oob_is_err=False).then_inc(sem["%s%d_%d" % (kind, s, u)], 16)
+
+    def dst_id(e):
+        rid, pid, _ = topo.addr(cores[e])
+        return DstId(rid=rid, pnc=pid)
+
+    sent = [0]
+
+    def send(s, parts):
+        tr = []
+        for codes, engines, lo, hi in parts:
+            src, dst = ("oc%d" % s, "ic%d" % r) if codes else ("op%d" % s, "ip%d" % r)
+            src, dst = T[src][:, lo:hi], T[dst][:, lo:hi]
+            if codes:
+                src, dst = src.bitcast(dt.uint8), dst.bitcast(dt.uint8)
+            sent[0] += len(engines)
+            tr.append(RemoteDMATransfer(dst_ids=[dst_id(slot[s])], dma_engine_mask=bits(engines),
+                                        remote_sem=sem["arr%d" % r], src=src, dst=dst))
+        g.remote_dma_fused(tr, local_sem=sem.sent)
+
+    g.wait_ge(sem.idx, 32)
+    g.wait_ge(sem.ma, 1)
+    gather("g", 0, 0)
+    g.wait_ge(sem.mb, 1)
+    gather("g", 0, 1)
+    g.wait_ge(sem.mx, 1)
+    gather("x", 0, 0)
+    gather("x", 0, 1)
+    g.wait_ge(sem.qg0, 1)
+    send(0, [(True, far_eng, 0, HALF)])
+    g.wait_ge(sem.m1, 1)
+    g.wait_ge(sem.tx, 16)
+    g.wait_ge(sem.ta, 48)
+    g.wait_ge(sem.tb, 16)
+    g.wait_ge(sem.tc, 32)
+    g.wait_ge(sem.td, 32)
+    gather("g", 1, 0)
+    gather("g", 1, 1)
+    g.wait_ge(sem.qx0, 1)
+    send(0, [(True, far_eng, HALF, COLS)])
+    send(0, [(False, far_eng, 0, COLS)])
+    g.wait_ge(sem.m2, 1)
+    gather("g", 2, 0)
+    gather("g", 2, 1)
+    g.wait_ge(sem.m3, 1)
+    gather("g", 3, 0)
+    g.wait_ge(sem.qx1, 1)
+    g.wait_ge(sem.qg1, 1)
+    send(1, [(True, far_eng, 0, COLS)])
+    send(1, [(False, far_eng, 0, COLS)])
+    gather("g", 3, 1)
+    g.wait_ge(sem.qx2, 1)
+    g.wait_ge(sem.qg2, 1)
+    send(2, [(True, near_eng, 0, MID), (True, far_eng, MID, COLS)])
+    send(2, [(False, near_eng, 0, COLS)])
+    g.wait_ge(sem.sent, sent[0])
+
+    v, a = g.vector, g.scalar
+
+    def views(kind, s, u, i, h):
+        t = 2 * u + i
+        lo, to = slice(QUADS * i, QUADS * (i + 1)), slice(QUADS * h, QUADS * (h + 1))
+        if kind == "g":
+            b, c = (T.rd0, u * GW) if s == 0 else (T["rj%d" % s], u * JW + XW)
+            return T["gt%d" % s][to, t:4 * HALF:4], b[lo, c + h * HALF:c + (h + 1) * HALF]
+        b, c = (T.rx0, u * XW) if s == 0 else (T["rj%d" % s], u * JW)
+        return T["xt%d" % s][to, 4 * XW * h + t:4 * XW * (h + 1):4], b[lo, c:c + XW]
+
+    count = {}
+
+    def vcopy(kind, s, u, i, h):
+        to, of = views(kind, s, u, i, h)
+        name = "v%s%d" % (kind, s)
+        count[name] = count.get(name, 0) + 1
+        v.tensor_copy(to, of).then_inc(sem[name], 1)
+
+    def acopy(kind, s, u, i, h):
+        to, of = views(kind, s, u, i, h)
+        name = "s%s%d" % (kind, s)
+        count[name] = count.get(name, 0) + 1
+        a.activation(to, of, ActivationFunctionType.Copy).then_inc(sem[name], 1)
+
+    def copies(kind, s, u):
+        name = "%s%d_%d" % (kind, s, u)
+        v.wait_ge(sem[name], 16)
+        a.wait_ge(sem[name], 16)
+        if s:
+            acopy("x", s, u, 1, 0)
+            acopy("x", s, u, 1, 1)
+            vcopy("x", s, u, 0, 0)
+            vcopy("x", s, u, 0, 1)
+        acopy(kind, s, u, 1, 1)
+        vcopy(kind, s, u, 0, 0)
+        vcopy(kind, s, u, 0, 1)
+        vcopy(kind, s, u, 1, 0)
+
+    def quant(kind, s):
+        if kind == "x":
+            v.wait_ge(sem["zx%d" % s], 2)
+        for q in "vs":
+            name = "%s%s%d" % (q, kind, s)
+            v.wait_ge(sem[name], count[name])
+        lo, hi = (0, HALF) if kind == "g" else (HALF, COLS)
+        tile = T["gt%d" % s] if kind == "g" else T["xt%d" % s]
+        v.quantize_mx(T["oc%d" % s][:, lo:hi], T["op%d" % s][:, lo:hi], tile[:]).then_inc(sem["q%s%d" % (kind, s)], 1)
+
+    def zeros_x(s):
+        v.memset(T["xt%d" % s][QUADS:128, 0:4 * XW], 0.0).then_inc(sem["zx%d" % s], 1)
+        v.memset(T["xt%d" % s][0:QUADS, 4 * XW:8 * XW], 0.0).then_inc(sem["zx%d" % s], 1)
+
+    v.memset(T.rd0[:, 0:GW], 0.0).then_inc(sem.ma, 1)
+    v.memset(T.rd0[:, GW:2 * GW], 0.0).then_inc(sem.mb, 1)
+    v.memset(T.rx0[:], 0.0).then_inc(sem.mx, 1)
+    v.memset(T.rj1[:], 0.0).then_inc(sem.m1, 1)
+    zeros_x(0)
+    copies("g", 0, 0)
+    zeros_x(1)
+    copies("g", 0, 1)
+    quant("g", 0)
+    v.memset(T.rj2[:], 0.0).then_inc(sem.m2, 1)
+    copies("x", 0, 0)
+    copies("x", 0, 1)
+    quant("x", 0)
+    v.memset(T.rj3[:], 0.0).then_inc(sem.m3, 1)
+    zeros_x(2)
+    zeros_x(3)
+    for s in (1, 2, 3):
+        copies("g", s, 0)
+        copies("g", s, 1)
+        quant("x", s)
+        quant("g", s)
+
+    pe = g.tensor
+    order = [early, r, near, late]
+    incs = {early: 3 * len(far_eng), late: 2 * len(far_eng), near: 2 * len(near_eng) + len(far_eng)}
+    for j, s in enumerate(order):
+        if s == r:
+            pe.wait_ge(sem.qx3, 1)
+            pe.wait_ge(sem.qg3, 1)
+            c, p = T.oc3, T.op3
+        else:
+            pe.wait_ge(sem["arr%d" % s], incs[s])
+            c, p = T["ic%d" % s], T["ip%d" % s]
+        for h in range(2):
+            w = slice(HALF + XW * h, HALF + XW * (h + 1))
+            m = pe.matmul_mx(T.acc[:, HALF * h:HALF * (h + 1)], c[:, w], p[:, w], c[:, 0:HALF], p[:, 0:HALF],
+                             j == 0, j == n - 1)
+            if j == n - 1:
+                m.then_inc(sem["mm%d" % h], 1)
+
+    v.wait_ge(sem.mm0, 1)
+    v.tensor_copy(T.ys[:, 0:HALF], T.acc[:, 0:HALF]).then_inc(sem.ev0, 1)
+    g.sync.wait_ge(sem.ev0, 1)
+    g.sync.dma_start(T.y[:, 0:HALF], T.ys[:, 0:HALF]).then_inc(sem.st0, 16)
+    g.sync.wait_ge(sem.st0, 16)
+    a.wait_ge(sem.mm1, 1)
+    a.activation(T.ys[:, HALF:GW], T.acc[:, HALF:GW], ActivationFunctionType.Copy).then_inc(sem.ev1, 1)
+    a.wait_ge(sem.ev1, 1)
+    a.dma_start(T.y[:, HALF:GW], T.ys[:, HALF:GW]).then_inc(sem.st1, 16)
+    a.wait_ge(sem.st1, 16)

@@ -4,9 +4,15 @@ from concourse.mybir import dt, ActivationFunctionType
 TOK, XW, GW = 1024, 128, 1024
 JW = XW + GW
 HALF = GW // 2
+QTR = HALF // 2
+BANK = 512
+MACHINE = 128
 QUADS = 64
-COLS = HALF + 2 * XW
+XC = 2 * XW
+COLS = XC + HALF
+LAST = XC + QTR
 MID = COLS // 2
+PIECE = COLS // 4
 
 SCRATCH = {
     "tab": ("dram", [TOK, JW], "bfloat16"),
@@ -14,24 +20,26 @@ SCRATCH = {
     "rx0": ("sbuf", [128, 2 * XW], "bfloat16"),
     "rd0": ("sbuf", [128, 2 * GW], "bfloat16"),
     "ys": ("sbuf", [128, GW], "float32"),
-    "acc": ("psum", [128, GW], "float32"),
+    "acc": ("psum", [128, 4 * BANK], "float32"),
+    "hc0": ("sbuf", [128, COLS], "float8_e4m3fn_x4"),
+    "hc1": ("sbuf", [128, COLS], "float8_e4m3fn_x4"),
 }
 for _s in range(4):
     if _s:
         SCRATCH["rj%d" % _s] = ("sbuf", [128, 2 * JW], "bfloat16")
     SCRATCH["gt%d" % _s] = ("sbuf", [128, 4 * HALF], "bfloat16")
-    SCRATCH["xt%d" % _s] = ("sbuf", [128, 8 * XW], "bfloat16")
+    SCRATCH["xt%d" % _s] = ("sbuf", [128, 4 * XC], "bfloat16")
     SCRATCH["oc%d" % _s] = ("sbuf", [128, COLS], "float8_e4m3fn_x4")
     SCRATCH["op%d" % _s] = ("sbuf", [128, COLS], "uint8")
     SCRATCH["ic%d" % _s] = ("sbuf", [128, COLS], "float8_e4m3fn_x4")
     SCRATCH["ip%d" % _s] = ("sbuf", [128, COLS], "uint8")
 
 SEMAPHORES = ["idx", "ta", "tb", "tc", "td", "tx", "ma", "mb", "mx", "m1", "m2", "m3", "sent",
-              "mm0", "mm1", "ev0", "ev1", "st0", "st1", "x0_0", "x0_1"]
+              "sta", "stb", "x0_0", "x0_1", "hin0", "hin1", "sk3", "vk3", "qk3"]
 for _s in range(4):
     SEMAPHORES += ["g%d_0" % _s, "g%d_1" % _s, "zx%d" % _s]
     SEMAPHORES += ["sg%d" % _s, "sx%d" % _s, "vg%d" % _s, "vx%d" % _s]
-    SEMAPHORES += ["qg%d" % _s, "qx%d" % _s, "arr%d" % _s]
+    SEMAPHORES += ["qg%d" % _s, "qx%d" % _s, "arr%d" % _s, "arb%d" % _s, "mm%d" % _s, "ev%d" % _s]
 
 
 def bits(engines):
@@ -39,9 +47,6 @@ def bits(engines):
 
 
 def rank_program(g, core, T, topo):
-    r = T.rank_of(core)
-    if r is None:
-        return
     cores = T.cores
     n = len(cores)
     sem = T.sem
@@ -53,14 +58,64 @@ def rank_program(g, core, T, topo):
         off = [e for e in range(n) if e not in here(s)]
         return off if here(s)[0] == s else off[::-1]
 
+    def helpers(s):
+        return [c for c in topo.cores_of(cores[s]) if c not in cores and topo.die(c) == topo.die(cores[s])]
+
+    def dst_id(c):
+        rid, pid, _ = topo.addr(c)
+        return DstId(rid=rid, pnc=pid)
+
+    def piece(to, name, engines, src, dst, lo, hi):
+        codes = src[1] == "c"
+        src, dst = T[src][:, lo:hi], T[dst][:, lo:hi]
+        if codes:
+            src, dst = src.bitcast(dt.uint8), dst.bitcast(dt.uint8)
+        return RemoteDMATransfer(dst_ids=[dst_id(to)], dma_engine_mask=bits(engines), remote_sem=sem[name],
+                                 src=src, dst=dst)
+
+    def detour(s):
+        to = cores[far_order(s)[0]]
+        return [(c, k) for c in helpers(s) for k in range(MACHINE)
+                if topo.mates(topo.chip(k), topo.chip(to)) and topo.die(k) == topo.die(c)
+                and topo.may_write(c, k) and topo.may_write(k, to)][0]
+
+    def hand_on(steps):
+        off = 0
+        for step in steps:
+            if len(step) == 2:
+                g.wait_ge(sem[step[0]], step[1])
+            else:
+                to, name, src, dst, lo, hi = step
+                eng = topo.engines(core, to)
+                g.remote_dma_fused([piece(to, name, eng, src, dst, lo, hi)], local_sem=sem.sent)
+                off += len(eng)
+        g.wait_ge(sem.sent, off)
+
+    r = T.rank_of(core)
+    if r is None:
+        for s in range(n):
+            aide, relay = detour(s)
+            first, second = [cores[e] for e in far_order(s)]
+            on, off = len(topo.engines(cores[s], aide)), len(topo.engines(aide, relay))
+            arr, arb, ic = "arr%d" % s, "arb%d" % s, "ic%d" % s
+            if core == aide:
+                hand_on([("hin0", on), (relay, "hin0", "hc0", "hc0", XC, LAST), (relay, "hin1", "hc0", "hc0", LAST, COLS),
+                         ("hin1", on - off), (second, arr, "hc1", ic, MID, LAST), (second, arb, "hc1", ic, LAST, COLS)])
+            if core == relay:
+                hand_on([("hin0", off), (first, arr, "hc0", ic, XC, LAST),
+                         ("hin1", off), (first, arr, "hc0", ic, LAST, COLS)])
+        return
+
     far = far_order(r)
     near = [e for e in here(r) if e != r][0]
     slot = far + [near, r]
     early = [s for s in far if far_order(s)[0] == r][0]
     late = [s for s in far if s != early][0]
+    aide = detour(r)[0]
 
     far_eng = topo.engines(core, cores[far[0]])
-    near_eng = [e for e in topo.engines(core, cores[near]) if e not in far_eng]
+    all_eng = topo.engines(core, cores[near])
+    on_eng = [e for e in all_eng if e not in far_eng]
 
     g.sync.dma_start(T.idx[0:QUADS, 0:15], T.pick[0:QUADS, 0:15]).then_inc(sem.idx, 16)
     g.scalar.dma_start(T.idx[QUADS:128, 0:15], T.pick[0:QUADS, 1:16]).then_inc(sem.idx, 16)
@@ -90,23 +145,24 @@ def rank_program(g, core, T, topo):
         g.indirect_dma_start(land, None, table, IndirectOffsetOnAxis(ap=T.idx[:, c:c + 1], axis=0),
                              bounds_check=TOK - 1, oob_is_err=False).then_inc(sem["%s%d_%d" % (kind, s, u)], 16)
 
-    def dst_id(e):
-        rid, pid, _ = topo.addr(cores[e])
-        return DstId(rid=rid, pnc=pid)
-
     sent = [0]
 
-    def send(s, parts):
+    def send(parts):
         tr = []
-        for codes, engines, lo, hi in parts:
-            src, dst = ("oc%d" % s, "ic%d" % r) if codes else ("op%d" % s, "ip%d" % r)
-            src, dst = T[src][:, lo:hi], T[dst][:, lo:hi]
-            if codes:
-                src, dst = src.bitcast(dt.uint8), dst.bitcast(dt.uint8)
+        for s, what, engines, lo, hi in parts:
             sent[0] += len(engines)
-            tr.append(RemoteDMATransfer(dst_ids=[dst_id(slot[s])], dma_engine_mask=bits(engines),
-                                        remote_sem=sem["arr%d" % r], src=src, dst=dst))
+            if what in "cp":
+                name = "arb%d" % r if lo == LAST else "arr%d" % r
+                tr.append(piece(cores[slot[s]], name, engines, "o%s%d" % (what, s), "i%s%d" % (what, r), lo, hi))
+            else:
+                tr.append(piece(aide, "hin%d" % s, engines, "oc%d" % s, "hc%d" % s, lo, hi))
         g.remote_dma_fused(tr, local_sem=sem.sent)
+
+    def ready(s):
+        g.wait_ge(sem["qx%d" % s], 1)
+        g.wait_ge(sem["qg%d" % s], 1)
+
+    fh, oh, oq = len(far_eng) // 2, len(on_eng) // 2, len(on_eng) // 4
 
     g.wait_ge(sem.idx, 32)
     g.wait_ge(sem.ma, 1)
@@ -117,7 +173,7 @@ def rank_program(g, core, T, topo):
     gather("x", 0, 0)
     gather("x", 0, 1)
     g.wait_ge(sem.qg0, 1)
-    send(0, [(True, far_eng, 0, HALF)])
+    send([(0, "h", all_eng, XC, COLS)])
     g.wait_ge(sem.m1, 1)
     g.wait_ge(sem.tx, 16)
     g.wait_ge(sem.ta, 48)
@@ -127,72 +183,71 @@ def rank_program(g, core, T, topo):
     gather("g", 1, 0)
     gather("g", 1, 1)
     g.wait_ge(sem.qx0, 1)
-    send(0, [(True, far_eng, HALF, COLS)])
-    send(0, [(False, far_eng, 0, COLS)])
+    send([(0, "c", far_eng, 0, XC)])
+    send([(0, "p", far_eng, 0, COLS)])
     g.wait_ge(sem.m2, 1)
     gather("g", 2, 0)
     gather("g", 2, 1)
+    ready(1)
+    send([(1, "c", far_eng, 0, MID), (1, "h", on_eng, MID, COLS)])
+    send([(1, "p", far_eng, 0, COLS)])
     g.wait_ge(sem.m3, 1)
     gather("g", 3, 0)
-    g.wait_ge(sem.qx1, 1)
-    g.wait_ge(sem.qg1, 1)
-    send(1, [(True, far_eng, 0, COLS)])
-    send(1, [(False, far_eng, 0, COLS)])
     gather("g", 3, 1)
-    g.wait_ge(sem.qx2, 1)
-    g.wait_ge(sem.qg2, 1)
-    send(2, [(True, near_eng, 0, MID), (True, far_eng, MID, COLS)])
-    send(2, [(False, near_eng, 0, COLS)])
+    ready(2)
+    send([(2, "c", all_eng, 0, LAST)])
+    send([(2, "p", all_eng, 0, COLS)])
+    send([(2, "c", all_eng, LAST, COLS)])
     g.wait_ge(sem.sent, sent[0])
 
     v, a = g.vector, g.scalar
 
-    def views(kind, s, u, i, h):
+    def views(kind, s, u, i, h, lo_c, hi_c):
         t = 2 * u + i
         lo, to = slice(QUADS * i, QUADS * (i + 1)), slice(QUADS * h, QUADS * (h + 1))
-        if kind == "g":
+        if kind != "x":
             b, c = (T.rd0, u * GW) if s == 0 else (T["rj%d" % s], u * JW + XW)
-            return T["gt%d" % s][to, t:4 * HALF:4], b[lo, c + h * HALF:c + (h + 1) * HALF]
+            return T["gt%d" % s][to, 4 * lo_c + t:4 * hi_c:4], b[lo, c + h * HALF + lo_c:c + h * HALF + hi_c]
         b, c = (T.rx0, u * XW) if s == 0 else (T["rj%d" % s], u * JW)
         return T["xt%d" % s][to, 4 * XW * h + t:4 * XW * (h + 1):4], b[lo, c:c + XW]
 
     count = {}
 
-    def vcopy(kind, s, u, i, h):
-        to, of = views(kind, s, u, i, h)
-        name = "v%s%d" % (kind, s)
+    def copy(q, kind, s, u, i, h, lo=0, hi=HALF):
+        to, of = views(kind, s, u, i, h, lo, hi)
+        name = "%s%s%d" % (q, kind, s)
         count[name] = count.get(name, 0) + 1
-        v.tensor_copy(to, of).then_inc(sem[name], 1)
+        if q == "v":
+            v.tensor_copy(to, of).then_inc(sem[name], 1)
+        else:
+            a.activation(to, of, ActivationFunctionType.Copy).then_inc(sem[name], 1)
 
-    def acopy(kind, s, u, i, h):
-        to, of = views(kind, s, u, i, h)
-        name = "s%s%d" % (kind, s)
-        count[name] = count.get(name, 0) + 1
-        a.activation(to, of, ActivationFunctionType.Copy).then_inc(sem[name], 1)
-
-    def copies(kind, s, u):
+    def landed(kind, s, u):
         name = "%s%d_%d" % (kind, s, u)
         v.wait_ge(sem[name], 16)
         a.wait_ge(sem[name], 16)
-        if s:
-            acopy("x", s, u, 1, 0)
-            acopy("x", s, u, 1, 1)
-            vcopy("x", s, u, 0, 0)
-            vcopy("x", s, u, 0, 1)
-        acopy(kind, s, u, 1, 1)
-        vcopy(kind, s, u, 0, 0)
-        vcopy(kind, s, u, 0, 1)
-        vcopy(kind, s, u, 1, 0)
 
-    def quant(kind, s):
+    def xcopies(s, u, queues):
+        for q, (i, h) in zip(queues, ((0, 0), (0, 1), (1, 0), (1, 1))):
+            copy(q, "x", s, u, i, h)
+
+    def gcopies(s, u, queues, kind="g", lo=0, hi=HALF):
+        for q, (i, h) in zip(queues, ((0, 0), (0, 1), (1, 0), (1, 1))):
+            copy(q, kind, s, u, i, h, lo, hi)
+
+    def quant(kind, s, lo=0, hi=HALF, after=""):
         if kind == "x":
             v.wait_ge(sem["zx%d" % s], 2)
-        for q in "vs":
-            name = "%s%s%d" % (q, kind, s)
-            v.wait_ge(sem[name], count[name])
-        lo, hi = (0, HALF) if kind == "g" else (HALF, COLS)
-        tile = T["gt%d" % s] if kind == "g" else T["xt%d" % s]
-        v.quantize_mx(T["oc%d" % s][:, lo:hi], T["op%d" % s][:, lo:hi], tile[:]).then_inc(sem["q%s%d" % (kind, s)], 1)
+        for k in after + kind:
+            for q in "vs":
+                name = "%s%s%d" % (q, k, s)
+                if name in count:
+                    v.wait_ge(sem[name], count[name])
+        if kind == "x":
+            tile, lo, hi = T["xt%d" % s][:], 0, XC
+        else:
+            tile, lo, hi = T["gt%d" % s][:, 4 * lo:4 * hi], XC + lo, XC + hi
+        v.quantize_mx(T["oc%d" % s][:, lo:hi], T["op%d" % s][:, lo:hi], tile).then_inc(sem["q%s%d" % (kind, s)], 1)
 
     def zeros_x(s):
         v.memset(T["xt%d" % s][QUADS:128, 0:4 * XW], 0.0).then_inc(sem["zx%d" % s], 1)
@@ -203,48 +258,70 @@ def rank_program(g, core, T, topo):
     v.memset(T.rx0[:], 0.0).then_inc(sem.mx, 1)
     v.memset(T.rj1[:], 0.0).then_inc(sem.m1, 1)
     zeros_x(0)
-    copies("g", 0, 0)
     zeros_x(1)
-    copies("g", 0, 1)
-    quant("g", 0)
     v.memset(T.rj2[:], 0.0).then_inc(sem.m2, 1)
-    copies("x", 0, 0)
-    copies("x", 0, 1)
+    landed("g", 0, 0)
+    gcopies(0, 0, "vvvs")
+    zeros_x(2)
+    landed("g", 0, 1)
+    gcopies(0, 1, "vvvs")
+    quant("g", 0)
+    zeros_x(3)
+    for u in range(2):
+        landed("x", 0, u)
+        xcopies(0, u, "vvss")
     quant("x", 0)
     v.memset(T.rj3[:], 0.0).then_inc(sem.m3, 1)
-    zeros_x(2)
-    zeros_x(3)
-    for s in (1, 2, 3):
-        copies("g", s, 0)
-        copies("g", s, 1)
+    for s in (1, 2):
+        for u in range(2):
+            landed("g", s, u)
+            xcopies(s, u, "vvvv")
+            gcopies(s, u, "vvss")
         quant("x", s)
         quant("g", s)
+    landed("g", 3, 0)
+    xcopies(3, 0, "vvvv")
+    gcopies(3, 0, "vvss")
+    landed("g", 3, 1)
+    xcopies(3, 1, "vvvv")
+    gcopies(3, 1, "vvss", "g", 0, QTR)
+    quant("x", 3)
+    quant("g", 3, 0, QTR)
+    gcopies(3, 1, "vvss", "k", QTR, HALF)
+    quant("k", 3, QTR, HALF)
 
     pe = g.tensor
-    order = [early, r, near, late]
-    incs = {early: 3 * len(far_eng), late: 2 * len(far_eng), near: 2 * len(near_eng) + len(far_eng)}
-    for j, s in enumerate(order):
-        if s == r:
-            pe.wait_ge(sem.qx3, 1)
-            pe.wait_ge(sem.qg3, 1)
-            c, p = T.oc3, T.op3
-        else:
-            pe.wait_ge(sem["arr%d" % s], incs[s])
-            c, p = T["ic%d" % s], T["ip%d" % s]
+    nf, na = len(far_eng), len(all_eng)
+    waits = {(early, 0): [("arr%d" % early, 4 * nf)], (early, 1): [],
+             (late, 0): [("arr%d" % late, 3 * nf)], (late, 1): [("arb%d" % late, nf)],
+             (near, 0): [("arr%d" % near, 2 * na)], (near, 1): [("arb%d" % near, na)],
+             (r, 0): [("qx3", 1), ("qg3", 1)], (r, 1): [("qk3", 1)]}
+    order = [(early, 0), (early, 1), (late, 0), (r, 0), (near, 0), (r, 1), (near, 1), (late, 1)]
+    for j, (s, c) in enumerate(order):
+        for name, k in waits[s, c]:
+            pe.wait_ge(sem[name], k)
+        c_, p_ = (T.oc3, T.op3) if s == r else (T["ic%d" % s], T["ip%d" % s])
+        first = all(cc != c for _, cc in order[:j])
+        last = all(cc != c for _, cc in order[j + 1:])
         for h in range(2):
-            w = slice(HALF + XW * h, HALF + XW * (h + 1))
-            m = pe.matmul_mx(T.acc[:, HALF * h:HALF * (h + 1)], c[:, w], p[:, w], c[:, 0:HALF], p[:, 0:HALF],
-                             j == 0, j == n - 1)
-            if j == n - 1:
-                m.then_inc(sem["mm%d" % h], 1)
+            q = 2 * c + h
+            w, m = slice(XW * h, XW * (h + 1)), slice(XC + QTR * c, XC + QTR * (c + 1))
+            mm = pe.matmul_mx(T.acc[:, BANK * q:BANK * q + QTR], c_[:, w], p_[:, w], c_[:, m], p_[:, m], first, last)
+            if last:
+                mm.then_inc(sem["mm%d" % q], 1)
 
-    v.wait_ge(sem.mm0, 1)
-    v.tensor_copy(T.ys[:, 0:HALF], T.acc[:, 0:HALF]).then_inc(sem.ev0, 1)
-    g.sync.wait_ge(sem.ev0, 1)
-    g.sync.dma_start(T.y[:, 0:HALF], T.ys[:, 0:HALF]).then_inc(sem.st0, 16)
-    g.sync.wait_ge(sem.st0, 16)
-    a.wait_ge(sem.mm1, 1)
-    a.activation(T.ys[:, HALF:GW], T.acc[:, HALF:GW], ActivationFunctionType.Copy).then_inc(sem.ev1, 1)
-    a.wait_ge(sem.ev1, 1)
-    a.dma_start(T.y[:, HALF:GW], T.ys[:, HALF:GW]).then_inc(sem.st1, 16)
-    a.wait_ge(sem.st1, 16)
+    for q in range(4):
+        c, h = divmod(q, 2)
+        cols = slice(HALF * h + QTR * c, HALF * h + QTR * (c + 1))
+        bank = T.acc[:, BANK * q:BANK * q + QTR]
+        if q % 2 == 0:
+            v.wait_ge(sem["mm%d" % q], 1)
+            v.tensor_copy(T.ys[:, cols], bank).then_inc(sem["ev%d" % q], 1)
+        else:
+            a.wait_ge(sem["mm%d" % q], 1)
+            a.activation(T.ys[:, cols], bank, ActivationFunctionType.Copy).then_inc(sem["ev%d" % q], 1)
+        queue, name = (g.sync, "sta") if q < 3 else (a, "stb")
+        queue.wait_ge(sem["ev%d" % q], 1)
+        queue.dma_start(T.y[:, cols], T.ys[:, cols]).then_inc(sem[name], 16)
+    g.sync.wait_ge(sem.sta, 48)
+    a.wait_ge(sem.stb, 16)

from concourse.bass import DstId, RemoteDMATransfer, IndirectOffsetOnAxis
from concourse.mybir import dt, ActivationFunctionType

TOK, XW, GW = 1024, 128, 1024
JW = XW + GW
HALF = GW // 2
QTR = HALF // 2
BANK = 512
MACHINE = 128
QUADS = 64
XC = 2 * XW
COLS = XC + HALF
LAST = XC + QTR
MID = COLS // 2
PIECE = COLS // 4

SCRATCH = {
    "tab": ("dram", [TOK, JW], "bfloat16"),
    "idx": ("sbuf", [128, 16], "int32"),
    "rx0": ("sbuf", [128, 2 * XW], "bfloat16"),
    "rd0": ("sbuf", [128, 2 * GW], "bfloat16"),
    "ys": ("sbuf", [128, GW], "float32"),
    "acc": ("psum", [128, 4 * BANK], "float32"),
    "hc0": ("sbuf", [128, COLS], "float8_e4m3fn_x4"),
    "hc1": ("sbuf", [128, COLS], "float8_e4m3fn_x4"),
}
for _s in range(4):
    if _s:
        SCRATCH["rj%d" % _s] = ("sbuf", [128, 2 * JW], "bfloat16")
    SCRATCH["gt%d" % _s] = ("sbuf", [128, 4 * HALF], "bfloat16")
    SCRATCH["xt%d" % _s] = ("sbuf", [128, 4 * XC], "bfloat16")
    SCRATCH["oc%d" % _s] = ("sbuf", [128, COLS], "float8_e4m3fn_x4")
    SCRATCH["op%d" % _s] = ("sbuf", [128, COLS], "uint8")
    SCRATCH["ic%d" % _s] = ("sbuf", [128, COLS], "float8_e4m3fn_x4")
    SCRATCH["ip%d" % _s] = ("sbuf", [128, COLS], "uint8")

SEMAPHORES = ["idx", "ta", "tb", "tc", "td", "tx", "ma", "mb", "mx", "m1", "m2", "m3", "sent",
              "sta", "stb", "x0_0", "x0_1", "hin0", "hin1", "sk3", "vk3", "qk3"]
for _s in range(4):
    SEMAPHORES += ["g%d_0" % _s, "g%d_1" % _s, "zx%d" % _s]
    SEMAPHORES += ["sg%d" % _s, "sx%d" % _s, "vg%d" % _s, "vx%d" % _s]
    SEMAPHORES += ["qg%d" % _s, "qx%d" % _s, "arr%d" % _s, "arb%d" % _s, "mm%d" % _s, "ev%d" % _s]


def bits(engines):
    return sum(1 << e for e in engines)


def rank_program(g, core, T, topo):
    cores = T.cores
    n = len(cores)
    sem = T.sem

    def here(s):
        return [e for e in range(n) if topo.chip(cores[e]) == topo.chip(cores[s])]

    def far_order(s):
        off = [e for e in range(n) if e not in here(s)]
        return off if here(s)[0] == s else off[::-1]

    def helpers(s):
        return [c for c in topo.cores_of(cores[s]) if c not in cores and topo.die(c) == topo.die(cores[s])]

    def dst_id(c):
        rid, pid, _ = topo.addr(c)
        return DstId(rid=rid, pnc=pid)

    def piece(to, name, engines, src, dst, lo, hi):
        codes = src[1] == "c"
        src, dst = T[src][:, lo:hi], T[dst][:, lo:hi]
        if codes:
            src, dst = src.bitcast(dt.uint8), dst.bitcast(dt.uint8)
        return RemoteDMATransfer(dst_ids=[dst_id(to)], dma_engine_mask=bits(engines), remote_sem=sem[name],
                                 src=src, dst=dst)

    def detour(s):
        to = cores[far_order(s)[0]]
        return [(c, k) for c in helpers(s) for k in range(MACHINE)
                if topo.mates(topo.chip(k), topo.chip(to)) and topo.die(k) == topo.die(c)
                and topo.may_write(c, k) and topo.may_write(k, to)][0]

    def hand_on(steps):
        off = 0
        for step in steps:
            if len(step) == 2:
                g.wait_ge(sem[step[0]], step[1])
            else:
                to, name, src, dst, lo, hi = step
                eng = topo.engines(core, to)
                g.remote_dma_fused([piece(to, name, eng, src, dst, lo, hi)], local_sem=sem.sent)
                off += len(eng)
        g.wait_ge(sem.sent, off)

    r = T.rank_of(core)
    if r is None:
        for s in range(n):
            aide, relay = detour(s)
            first, second = [cores[e] for e in far_order(s)]
            on, off = len(topo.engines(cores[s], aide)), len(topo.engines(aide, relay))
            arr, arb, ic = "arr%d" % s, "arb%d" % s, "ic%d" % s
            if core == aide:
                hand_on([("hin0", on), (relay, "hin0", "hc0", "hc0", XC, LAST), (relay, "hin1", "hc0", "hc0", LAST, COLS),
                         ("hin1", on - off), (second, arr, "hc1", ic, MID, LAST), (second, arb, "hc1", ic, LAST, COLS)])
            if core == relay:
                hand_on([("hin0", off), (first, arr, "hc0", ic, XC, LAST),
                         ("hin1", off), (first, arr, "hc0", ic, LAST, COLS)])
        return

    far = far_order(r)
    near = [e for e in here(r) if e != r][0]
    slot = far + [near, r]
    early = [s for s in far if far_order(s)[0] == r][0]
    late = [s for s in far if s != early][0]
    aide = detour(r)[0]

    far_eng = topo.engines(core, cores[far[0]])
    all_eng = topo.engines(core, cores[near])
    on_eng = [e for e in all_eng if e not in far_eng]

    g.sync.dma_start(T.idx[0:QUADS, 0:15], T.pick[0:QUADS, 0:15]).then_inc(sem.idx, 16)
    g.scalar.dma_start(T.idx[QUADS:128, 0:15], T.pick[0:QUADS, 1:16]).then_inc(sem.idx, 16)

    def tab_dy(j, name):
        g.sync.dma_start(T.tab[128 * j:128 * j + 128, XW:JW], T.dy[128 * j:128 * j + 128, :]).then_inc(sem[name], 16)

    g.dma_start(T.tab[:, 0:XW], T.x[:, :]).then_inc(sem.tx, 16)
    for j in (0, 1, 2):
        tab_dy(j, "ta")
    tab_dy(3, "tb")
    g.sync.wait_ge(sem.ta, 48)
    tab_dy(4, "tc")
    tab_dy(5, "tc")
    g.sync.wait_ge(sem.tb, 16)
    tab_dy(6, "td")
    tab_dy(7, "td")

    def gather(kind, s, u):
        c = 4 * slot[s] + 2 * u
        if kind == "x":
            land, table = T.rx0[:, u * XW:(u + 1) * XW], T.x[:]
        elif s == 0:
            land, table = T.rd0[:, u * GW:(u + 1) * GW], T.dy[:]
        else:
            land, table = T["rj%d" % s][:, u * JW:(u + 1) * JW], T.tab[:]
        g.indirect_dma_start(land, None, table, IndirectOffsetOnAxis(ap=T.idx[:, c:c + 1], axis=0),
                             bounds_check=TOK - 1, oob_is_err=False).then_inc(sem["%s%d_%d" % (kind, s, u)], 16)

    sent = [0]

    def send(parts):
        tr = []
        for s, what, engines, lo, hi in parts:
            sent[0] += len(engines)
            if what in "cp":
                name = "arb%d" % r if lo == LAST else "arr%d" % r
                tr.append(piece(cores[slot[s]], name, engines, "o%s%d" % (what, s), "i%s%d" % (what, r), lo, hi))
            else:
                tr.append(piece(aide, "hin%d" % s, engines, "oc%d" % s, "hc%d" % s, lo, hi))
        g.remote_dma_fused(tr, local_sem=sem.sent)

    def ready(s):
        g.wait_ge(sem["qx%d" % s], 1)
        g.wait_ge(sem["qg%d" % s], 1)

    fh, oh, oq = len(far_eng) // 2, len(on_eng) // 2, len(on_eng) // 4

    g.wait_ge(sem.idx, 32)
    g.wait_ge(sem.ma, 1)
    gather("g", 0, 0)
    g.wait_ge(sem.mb, 1)
    gather("g", 0, 1)
    g.wait_ge(sem.mx, 1)
    gather("x", 0, 0)
    gather("x", 0, 1)
    g.wait_ge(sem.qg0, 1)
    send([(0, "h", all_eng, XC, COLS)])
    g.wait_ge(sem.m1, 1)
    g.wait_ge(sem.tx, 16)
    g.wait_ge(sem.ta, 48)
    g.wait_ge(sem.tb, 16)
    g.wait_ge(sem.tc, 32)
    g.wait_ge(sem.td, 32)
    gather("g", 1, 0)
    gather("g", 1, 1)
    g.wait_ge(sem.qx0, 1)
    send([(0, "c", far_eng, 0, XC)])
    send([(0, "p", far_eng, 0, COLS)])
    g.wait_ge(sem.m2, 1)
    gather("g", 2, 0)
    gather("g", 2, 1)
    ready(1)
    send([(1, "c", far_eng, 0, MID), (1, "h", on_eng, MID, COLS)])
    send([(1, "p", far_eng, 0, COLS)])
    g.wait_ge(sem.m3, 1)
    gather("g", 3, 0)
    gather("g", 3, 1)
    ready(2)
    send([(2, "c", all_eng, 0, LAST)])
    send([(2, "p", all_eng, 0, COLS)])
    send([(2, "c", all_eng, LAST, COLS)])
    g.wait_ge(sem.sent, sent[0])

    v, a = g.vector, g.scalar

    def views(kind, s, u, i, h, lo_c, hi_c):
        t = 2 * u + i
        lo, to = slice(QUADS * i, QUADS * (i + 1)), slice(QUADS * h, QUADS * (h + 1))
        if kind != "x":
            b, c = (T.rd0, u * GW) if s == 0 else (T["rj%d" % s], u * JW + XW)
            return T["gt%d" % s][to, 4 * lo_c + t:4 * hi_c:4], b[lo, c + h * HALF + lo_c:c + h * HALF + hi_c]
        b, c = (T.rx0, u * XW) if s == 0 else (T["rj%d" % s], u * JW)
        return T["xt%d" % s][to, 4 * XW * h + t:4 * XW * (h + 1):4], b[lo, c:c + XW]

    count = {}

    def copy(q, kind, s, u, i, h, lo=0, hi=HALF):
        to, of = views(kind, s, u, i, h, lo, hi)
        name = "%s%s%d" % (q, kind, s)
        count[name] = count.get(name, 0) + 1
        if q == "v":
            v.tensor_copy(to, of).then_inc(sem[name], 1)
        else:
            a.activation(to, of, ActivationFunctionType.Copy).then_inc(sem[name], 1)

    def landed(kind, s, u):
        name = "%s%d_%d" % (kind, s, u)
        v.wait_ge(sem[name], 16)
        a.wait_ge(sem[name], 16)

    def xcopies(s, u, queues):
        for q, (i, h) in zip(queues, ((0, 0), (0, 1), (1, 0), (1, 1))):
            copy(q, "x", s, u, i, h)

    def gcopies(s, u, queues, kind="g", lo=0, hi=HALF):
        for q, (i, h) in zip(queues, ((0, 0), (0, 1), (1, 0), (1, 1))):
            copy(q, kind, s, u, i, h, lo, hi)

    def quant(kind, s, lo=0, hi=HALF, after=""):
        if kind == "x":
            v.wait_ge(sem["zx%d" % s], 2)
        for k in after + kind:
            for q in "vs":
                name = "%s%s%d" % (q, k, s)
                if name in count:
                    v.wait_ge(sem[name], count[name])
        if kind == "x":
            tile, lo, hi = T["xt%d" % s][:], 0, XC
        else:
            tile, lo, hi = T["gt%d" % s][:, 4 * lo:4 * hi], XC + lo, XC + hi
        v.quantize_mx(T["oc%d" % s][:, lo:hi], T["op%d" % s][:, lo:hi], tile).then_inc(sem["q%s%d" % (kind, s)], 1)

    def zeros_x(s):
        v.memset(T["xt%d" % s][QUADS:128, 0:4 * XW], 0.0).then_inc(sem["zx%d" % s], 1)
        v.memset(T["xt%d" % s][0:QUADS, 4 * XW:8 * XW], 0.0).then_inc(sem["zx%d" % s], 1)

    v.memset(T.rd0[:, 0:GW], 0.0).then_inc(sem.ma, 1)
    v.memset(T.rd0[:, GW:2 * GW], 0.0).then_inc(sem.mb, 1)
    v.memset(T.rx0[:], 0.0).then_inc(sem.mx, 1)
    v.memset(T.rj1[:], 0.0).then_inc(sem.m1, 1)
    zeros_x(0)
    zeros_x(1)
    v.memset(T.rj2[:], 0.0).then_inc(sem.m2, 1)
    landed("g", 0, 0)
    gcopies(0, 0, "vvvs")
    zeros_x(2)
    landed("g", 0, 1)
    gcopies(0, 1, "vvvs")
    quant("g", 0)
    zeros_x(3)
    for u in range(2):
        landed("x", 0, u)
        xcopies(0, u, "vvss")
    quant("x", 0)
    v.memset(T.rj3[:], 0.0).then_inc(sem.m3, 1)
    for s in (1, 2):
        for u in range(2):
            landed("g", s, u)
            xcopies(s, u, "vvvv")
            gcopies(s, u, "vvss")
        quant("x", s)
        quant("g", s)
    landed("g", 3, 0)
    xcopies(3, 0, "vvvv")
    gcopies(3, 0, "vvss")
    landed("g", 3, 1)
    xcopies(3, 1, "vvvv")
    gcopies(3, 1, "vvss", "g", 0, QTR)
    quant("x", 3)
    quant("g", 3, 0, QTR)
    gcopies(3, 1, "vvss", "k", QTR, HALF)
    quant("k", 3, QTR, HALF)

    pe = g.tensor
    nf, na = len(far_eng), len(all_eng)
    waits = {(early, 0): [("arr%d" % early, 4 * nf)], (early, 1): [],
             (late, 0): [("arr%d" % late, 3 * nf)], (late, 1): [("arb%d" % late, nf)],
             (near, 0): [("arr%d" % near, 2 * na)], (near, 1): [("arb%d" % near, na)],
             (r, 0): [("qx3", 1), ("qg3", 1)], (r, 1): [("qk3", 1)]}
    order = [(early, 0), (early, 1), (late, 0), (r, 0), (near, 0), (r, 1), (near, 1), (late, 1)]
    for j, (s, c) in enumerate(order):
        for name, k in waits[s, c]:
            pe.wait_ge(sem[name], k)
        c_, p_ = (T.oc3, T.op3) if s == r else (T["ic%d" % s], T["ip%d" % s])
        first = all(cc != c for _, cc in order[:j])
        last = all(cc != c for _, cc in order[j + 1:])
        for h in range(2):
            q = 2 * c + h
            w, m = slice(XW * h, XW * (h + 1)), slice(XC + QTR * c, XC + QTR * (c + 1))
            mm = pe.matmul_mx(T.acc[:, BANK * q:BANK * q + QTR], c_[:, w], p_[:, w], c_[:, m], p_[:, m], first, last)
            if last:
                mm.then_inc(sem["mm%d" % q], 1)

    for q in range(4):
        c, h = divmod(q, 2)
        cols = slice(HALF * h + QTR * c, HALF * h + QTR * (c + 1))
        bank = T.acc[:, BANK * q:BANK * q + QTR]
        if q % 2 == 0:
            v.wait_ge(sem["mm%d" % q], 1)
            v.tensor_copy(T.ys[:, cols], bank).then_inc(sem["ev%d" % q], 1)
        else:
            a.wait_ge(sem["mm%d" % q], 1)
            a.activation(T.ys[:, cols], bank, ActivationFunctionType.Copy).then_inc(sem["ev%d" % q], 1)
        queue, name = (g.sync, "sta") if q < 3 else (a, "stb")
        queue.wait_ge(sem["ev%d" % q], 1)
        queue.dma_start(T.y[:, cols], T.ys[:, cols]).then_inc(sem[name], 16)
    g.sync.wait_ge(sem.sta, 48)
    a.wait_ge(sem.stb, 16)
